import numpy as np
import ml_dtypes


def mxq(x, axis, fmt="e4m3"):
    dtype, down = {"e4m3": (ml_dtypes.float8_e4m3fn, 7), "e5m2": (ml_dtypes.float8_e5m2, 14)}[fmt]
    v = np.moveaxis(np.asarray(x, np.float32).astype(ml_dtypes.bfloat16).astype(np.float64), axis, -1)
    blocks = v.reshape(v.shape[:-1] + (-1, 32))
    amax = np.abs(blocks).max(-1, keepdims=True)
    byte = np.maximum(np.where(amax > 0, np.frexp(amax)[1] - 1 + 127, 0) - down, 1)
    scale = np.exp2(byte - 127.0)
    codes = (blocks / scale).astype(np.float32).astype(dtype).astype(np.float64)
    return np.moveaxis((codes * scale).reshape(v.shape), -1, axis)


WIDE = False


def mx_kscale(k):
    if not WIDE:
        return np.ones(k)
    levels = np.array([10, -10, 5, -5, 0])
    if k % 512:
        return np.exp2(np.random.permutation(np.resize(levels, k // 32))).repeat(32)
    a = np.empty((k // 512, 16))
    for p in range(k // 512):
        a[p, :8] = np.random.permutation(np.resize(levels, 8))
        for g in range(8):
            far = levels[np.abs(levels - a[p, g]) >= 10]
            a[p, g + 8] = far[np.random.randint(len(far))]
    return np.exp2(a.ravel()).repeat(32)


def f64(x):
    return np.asarray(x).astype(np.float64)


def striped(idx):
    return np.tile(idx.reshape(-1, 16).T, (8, 1)).astype(np.uint16)


def unstriped(offs):
    return offs[:16].T.reshape(-1).astype(np.int64)


def silu(v):
    return v / (1.0 + np.exp(-np.maximum(v, -700.0)))


K, T, S, H, N = 1024, 1024, 512, 512, 512


def setup_inputs():
    n = np.random.standard_normal
    s = mx_kscale(K)[:, None]
    u = mx_kscale(H)
    return {
        "xT": (n((K, S)) * s).astype(np.float32),
        "w1": (n((K, H)) / np.sqrt(K) / s * u).astype(np.float32),
        "w2": (n((H, N)) / np.sqrt(H) / u[:, None]).astype(np.float32),
        "gate": np.tile(np.random.uniform(0.2, 1.0, S), (N, 1)).astype(np.float32),
        "offs": striped(np.sort(np.random.permutation(T)[:S])),
    }


def reference(xT, w1, w2, gate, offs):
    idx = unstriped(offs)
    xq = mxq(f64(xT), 0, "e4m3")
    h = silu(mxq(f64(w1), 0, "e4m3").T @ xq)
    y = mxq(f64(w2), 0, "e4m3").T @ mxq(h, 0, "e4m3")
    out = np.zeros((N, T))
    out[:, idx] = f64(gate) * y
    return out

@@ -1,0 +1,184 @@
+from contextlib import ExitStack
+
+import concourse.mybir as mybir
+
+K, T, S, H, N = 1024, 1024, 512, 512, 512
+FLOPS = 2 * S * (K * H + H * N)
+BYTES = 4 * (K * S + K * H + H * N + S + N * T) + 2 * 128 * (S // 16)
+
+F32 = mybir.dt.float32
+BF16 = mybir.dt.bfloat16
+U32 = mybir.dt.uint32
+U16 = mybir.dt.uint16
+U8 = mybir.dt.uint8
+I32 = mybir.dt.int32
+FP8X4 = mybir.dt.float8_e4m3fn_x4
+SILU = mybir.ActivationFunctionType.Silu
+MULT = mybir.AluOpType.mult
+
+P = 128
+CH = 128
+HALF = 256
+
+
+def tile_picked_place_mlp_silu_srt_l_kernel(tc, xT, w1, w2, gate, offs, out):
+    nc = tc.nc
+    with ExitStack() as ctx:
+        sb = ctx.enter_context(tc.tile_pool(name="sb", bufs=1))
+        ps = ctx.enter_context(tc.psum_pool(name="ps", bufs=1))
+
+        def tile(shape, dt, name, align=64):
+            return sb.tile(shape, dt, name=name, align_bytes=align)
+
+        offsets = sb.tile([128, S // 16], U16, name="offsets")
+        gate_sb = tile([P, S], F32, "gate_sb")
+        w1_raw = [tile([P, 4, H], F32, f"w1_raw{k}") for k in range(2)]
+        w1_bf = [tile([P, 4 * H], BF16, f"w1_bf{k}") for k in range(2)]
+        w1_c = [tile([P, H], U32, f"w1_c{k}") for k in range(2)]
+        w1_s = [tile([P, H], U8, f"w1_s{k}") for k in range(2)]
+        x_raw = [[tile([P, 4, HALF], F32, f"x_raw{t}{k}") for k in range(2)] for t in range(2)]
+        x_bf = [[tile([P, CH, 4], BF16, f"x_bf{c}{k}") for k in range(2)] for c in range(4)]
+        x_c = [[tile([P, CH], U32, f"x_c{c}{k}") for k in range(2)] for c in range(4)]
+        x_s = [[tile([P, CH], U8, f"x_s{c}{k}") for k in range(2)] for c in range(4)]
+        w2_raw = [tile([P, 4, HALF], F32, f"w2_raw{m}") for m in range(2)]
+        w2_bf = [tile([P, HALF, 4], BF16, f"w2_bf{m}") for m in range(2)]
+        w2_c = [tile([P, HALF], U32, f"w2_c{m}") for m in range(2)]
+        w2_s = [tile([P, HALF], U8, f"w2_s{m}") for m in range(2)]
+        h_bf = [tile([P, CH, 4], BF16, f"h_bf{c}") for c in range(4)]
+        h_c = [tile([P, HALF], U32, f"h_c{t}") for t in range(2)]
+        h_s = [tile([P, HALF], U8, f"h_s{t}") for t in range(2)]
+        win = [tile([P, T], F32, f"win{m}") for m in range(4)]
+        warm = tile([P, 1], F32, "warm")
+        warm_out = tile([P, 1], F32, "warm_out")
+
+        def load_x(t, k):
+            nc.sync.dma_start(
+                out=x_raw[t][k][:],
+                in_=xT[k * 512 : (k + 1) * 512, t * HALF : (t + 1) * HALF].rearrange("(p j) n -> p j n", j=4),
+            )
+
+        def load_w2(m):
+            nc.sync.dma_start(
+                out=w2_raw[m][:], in_=w2[:, m * HALF : (m + 1) * HALF].rearrange("(p j) n -> p j n", j=4)
+            )
+
+        for k in range(2):
+            nc.sync.dma_start(
+                out=w1_raw[k][:], in_=w1[k * 512 : (k + 1) * 512, :].rearrange("(p j) n -> p j n", j=4)
+            )
+        load_x(0, 0)
+        load_x(0, 1)
+        load_w2(0)
+        nc.sync.dma_start(offsets[:], offs)
+        nc.sync.dma_start(out=gate_sb[:], in_=gate[0:P, :])
+        load_x(1, 0)
+        load_x(1, 1)
+        load_w2(1)
+
+        nc.gpsimd.memset(warm[:], 0.0)
+        nc.scalar.activation(warm_out[:], warm[:], SILU)
+        for m in range(4):
+            nc.vector.memset(win[m][:].bitcast(I32), 0)
+
+        def w1_copy(k, copy, a, b):
+            copy(
+                w1_bf[k][:].rearrange("p (t m j) -> p m t j", t=4, j=4)[:, a:b],
+                w1_raw[k][:].rearrange("p j (m t) -> p m t j", t=4)[:, a:b],
+            )
+
+        for k in range(2):
+            w1_copy(k, nc.scalar.copy, 64, 128)
+            w1_copy(k, nc.vector.tensor_copy, 0, 64)
+            nc.vector.quantize_mx(out=w1_c[k][:].bitcast(FP8X4), scales=w1_s[k][:], in_=w1_bf[k][:])
+
+        def x_prep(t, k):
+            for copy, c in ((nc.scalar.copy, 1), (nc.vector.tensor_copy, 0)):
+                copy(
+                    x_bf[2 * t + c][k][:],
+                    x_raw[t][k][:].rearrange("p j n -> p n j")[:, c * CH : (c + 1) * CH],
+                )
+            for c in (2 * t, 2 * t + 1):
+                nc.vector.quantize_mx(
+                    out=x_c[c][k][:].bitcast(FP8X4),
+                    scales=x_s[c][k][:],
+                    in_=x_bf[c][k][:].rearrange("p n j -> p (n j)"),
+                )
+
+        def w2_prep(m):
+            nc.scalar.copy(w2_bf[m][:, 0:CH], w2_raw[m][:].rearrange("p j n -> p n j")[:, 0:CH])
+            nc.vector.tensor_copy(w2_bf[m][:, CH:HALF], w2_raw[m][:].rearrange("p j n -> p n j")[:, CH:HALF])
+            nc.vector.quantize_mx(
+                out=w2_c[m][:].bitcast(FP8X4),
+                scales=w2_s[m][:],
+                in_=w2_bf[m][:].rearrange("p n j -> p (n j)"),
+            )
+
+        def stage1(c):
+            acc = ps.tile([P, 4, CH], F32, name=f"h_acc{c}")
+            for t in range(4):
+                for k in range(2):
+                    nc.tensor.matmul_mx(
+                        out=acc[:, t, :],
+                        lhsT=w1_c[k][:, t * P : (t + 1) * P].bitcast(FP8X4),
+                        lhsT_scale=w1_s[k][:, t * P : (t + 1) * P],
+                        rhs=x_c[c][k][:].bitcast(FP8X4),
+                        rhs_scale=x_s[c][k][:],
+                        start=(k == 0),
+                        stop=(k == 1),
+                    )
+            nc.scalar.activation(h_bf[c][:], acc[:].rearrange("p t n -> p n t"), SILU)
+
+        def h_quant(c):
+            a = (c % 2) * CH
+            nc.vector.quantize_mx(
+                out=h_c[c // 2][:, a : a + CH].bitcast(FP8X4),
+                scales=h_s[c // 2][:, a : a + CH],
+                in_=h_bf[c][:].rearrange("p n t -> p (n t)"),
+            )
+
+        def y_mm(acc, ms, t, a, n):
+            for u, m in enumerate(ms):
+                nc.tensor.matmul_mx(
+                    out=acc[:, u, :],
+                    lhsT=w2_c[m // 2][:, (m % 2) * P : (m % 2 + 1) * P].bitcast(FP8X4),
+                    lhsT_scale=w2_s[m // 2][:, (m % 2) * P : (m % 2 + 1) * P],
+                    rhs=h_c[t][:, a : a + n].bitcast(FP8X4),
+                    rhs_scale=h_s[t][:, a : a + n],
+                    start=True,
+                    stop=True,
+                )
+
+        def stage2(name, ms, t, a, n):
+            acc = ps.tile([P, len(ms), n], F32, name=f"y_acc{name}")
+            y_sb = sb.tile([P, len(ms), n], F32, name=f"y_sb{name}", align_bytes=64)
+            y_mm(acc, ms, t, a, n)
+            nc.scalar.copy(y_sb[:], acc[:])
+            j0 = t * HALF + a
+            for u, m in enumerate(ms):
+                nc.vector.tensor_tensor(
+                    win[m][:].indirect(offsets[:, j0 // 16 : (j0 + n) // 16]),
+                    y_sb[:, u, :],
+                    gate_sb[:, j0 : j0 + n],
+                    MULT,
+                )
+
+        x_prep(0, 0)
+        x_prep(0, 1)
+        stage1(0)
+        stage1(1)
+        w2_prep(0)
+        h_quant(0)
+        h_quant(1)
+        stage2("a", (0, 1), 0, 0, HALF)
+        x_prep(1, 0)
+        x_prep(1, 1)
+        stage1(2)
+        stage1(3)
+        w2_prep(1)
+        stage2("b", (2, 3), 0, 0, HALF)
+        h_quant(2)
+        stage2("c", (0, 1, 2, 3), 1, 0, CH)
+        h_quant(3)
+        stage2("d", (0, 1, 2, 3), 1, CH, CH)
+        for m in range(4):
+            nc.sync.dma_start(out=out[m * P : (m + 1) * P, :], in_=win[m][:])

@@ -27,8 +27,8 @@ def tile_picked_place_mlp_silu_srt_l_kernel(tc, xT, w1, w2, gate, offs, out):
         sb = ctx.enter_context(tc.tile_pool(name="sb", bufs=1))
         ps = ctx.enter_context(tc.psum_pool(name="ps", bufs=1))
 
-        def tile(shape, dt, name, align=64):
-            return sb.tile(shape, dt, name=name, align_bytes=align)
+        def tile(shape, dt, name):
+            return sb.tile(shape, dt, name=name, align_bytes=64)
 
         offsets = sb.tile([128, S // 16], U16, name="offsets")
         gate_sb = tile([P, S], F32, "gate_sb")
@@ -36,49 +36,39 @@ def tile_picked_place_mlp_silu_srt_l_kernel(tc, xT, w1, w2, gate, offs, out):
         w1_bf = [tile([P, 4 * H], BF16, f"w1_bf{k}") for k in range(2)]
         w1_c = [tile([P, H], U32, f"w1_c{k}") for k in range(2)]
         w1_s = [tile([P, H], U8, f"w1_s{k}") for k in range(2)]
-        x_raw = [[tile([P, 4, HALF], F32, f"x_raw{t}{k}") for k in range(2)] for t in range(2)]
-        x_bf = [[tile([P, CH, 4], BF16, f"x_bf{c}{k}") for k in range(2)] for c in range(4)]
-        x_c = [[tile([P, CH], U32, f"x_c{c}{k}") for k in range(2)] for c in range(4)]
-        x_s = [[tile([P, CH], U8, f"x_s{c}{k}") for k in range(2)] for c in range(4)]
-        w2_raw = [tile([P, 4, HALF], F32, f"w2_raw{m}") for m in range(2)]
-        w2_bf = [tile([P, HALF, 4], BF16, f"w2_bf{m}") for m in range(2)]
-        w2_c = [tile([P, HALF], U32, f"w2_c{m}") for m in range(2)]
-        w2_s = [tile([P, HALF], U8, f"w2_s{m}") for m in range(2)]
+        x_raw = [tile([P, 4, S], F32, f"x_raw{k}") for k in range(2)]
+        x_bf = [tile([P, S, 4], BF16, f"x_bf{k}") for k in range(2)]
+        x_c = [tile([P, S], U32, f"x_c{k}") for k in range(2)]
+        x_s = [tile([P, S], U8, f"x_s{k}") for k in range(2)]
+        w2_raw = tile([P, 4, N], F32, "w2_raw")
+        w2_bf = tile([P, N, 4], BF16, "w2_bf")
+        w2_c = tile([P, N], U32, "w2_c")
+        w2_s = tile([P, N], U8, "w2_s")
         h_bf = [tile([P, CH, 4], BF16, f"h_bf{c}") for c in range(4)]
-        h_c = [tile([P, HALF], U32, f"h_c{t}") for t in range(2)]
-        h_s = [tile([P, HALF], U8, f"h_s{t}") for t in range(2)]
+        h_c = tile([P, S], U32, "h_c")
+        h_s = tile([P, S], U8, "h_s")
+        y_sb = [tile([P, S], F32, f"y_sb{m}") for m in range(4)]
         win = [tile([P, T], F32, f"win{m}") for m in range(4)]
         warm = tile([P, 1], F32, "warm")
         warm_out = tile([P, 1], F32, "warm_out")
 
-        def load_x(t, k):
-            nc.sync.dma_start(
-                out=x_raw[t][k][:],
-                in_=xT[k * 512 : (k + 1) * 512, t * HALF : (t + 1) * HALF].rearrange("(p j) n -> p j n", j=4),
-            )
-
-        def load_w2(m):
-            nc.sync.dma_start(
-                out=w2_raw[m][:], in_=w2[:, m * HALF : (m + 1) * HALF].rearrange("(p j) n -> p j n", j=4)
-            )
+        def load(dst, rows):
+            nc.sync.dma_start(out=dst[:], in_=rows.rearrange("(p j) n -> p j n", j=4))
 
         for k in range(2):
-            nc.sync.dma_start(
-                out=w1_raw[k][:], in_=w1[k * 512 : (k + 1) * 512, :].rearrange("(p j) n -> p j n", j=4)
-            )
-        load_x(0, 0)
-        load_x(0, 1)
-        load_w2(0)
+            load(w1_raw[k], w1[k * 512 : (k + 1) * 512, :])
+        for k in range(2):
+            load(x_raw[k], xT[k * 512 : (k + 1) * 512, :])
+        load(w2_raw, w2)
         nc.sync.dma_start(offsets[:], offs)
         nc.sync.dma_start(out=gate_sb[:], in_=gate[0:P, :])
-        load_x(1, 0)
-        load_x(1, 1)
-        load_w2(1)
 
         nc.gpsimd.memset(warm[:], 0.0)
         nc.scalar.activation(warm_out[:], warm[:], SILU)
         for m in range(4):
             nc.vector.memset(win[m][:].bitcast(I32), 0)
+
+        act, vec = nc.scalar.copy, nc.vector.tensor_copy
 
         def w1_copy(k, copy, a, b):
             copy(
@@ -86,99 +76,83 @@ def tile_picked_place_mlp_silu_srt_l_kernel(tc, xT, w1, w2, gate, offs, out):
                 w1_raw[k][:].rearrange("p j (m t) -> p m t j", t=4)[:, a:b],
             )
 
-        for k in range(2):
-            w1_copy(k, nc.scalar.copy, 64, 128)
-            w1_copy(k, nc.vector.tensor_copy, 0, 64)
-            nc.vector.quantize_mx(out=w1_c[k][:].bitcast(FP8X4), scales=w1_s[k][:], in_=w1_bf[k][:])
+        def lay(dst, raw, copy, a, b):
+            copy(dst[:, a:b], raw[:].rearrange("p j n -> p n j")[:, a:b])
 
-        def x_prep(t, k):
-            for copy, c in ((nc.scalar.copy, 1), (nc.vector.tensor_copy, 0)):
-                copy(
-                    x_bf[2 * t + c][k][:],
-                    x_raw[t][k][:].rearrange("p j n -> p n j")[:, c * CH : (c + 1) * CH],
-                )
-            for c in (2 * t, 2 * t + 1):
-                nc.vector.quantize_mx(
-                    out=x_c[c][k][:].bitcast(FP8X4),
-                    scales=x_s[c][k][:],
-                    in_=x_bf[c][k][:].rearrange("p n j -> p (n j)"),
-                )
-
-        def w2_prep(m):
-            nc.scalar.copy(w2_bf[m][:, 0:CH], w2_raw[m][:].rearrange("p j n -> p n j")[:, 0:CH])
-            nc.vector.tensor_copy(w2_bf[m][:, CH:HALF], w2_raw[m][:].rearrange("p j n -> p n j")[:, CH:HALF])
+        def quant(codes, scales, src, a, b):
             nc.vector.quantize_mx(
-                out=w2_c[m][:].bitcast(FP8X4),
-                scales=w2_s[m][:],
-                in_=w2_bf[m][:].rearrange("p n j -> p (n j)"),
+                out=codes[:, a:b].bitcast(FP8X4),
+                scales=scales[:, a:b],
+                in_=src[:, a:b].rearrange("p n j -> p (n j)"),
             )
 
-        def stage1(c):
-            acc = ps.tile([P, 4, CH], F32, name=f"h_acc{c}")
+        for k in range(2):
+            w1_copy(k, act, 64, 96)
+            w1_copy(k, vec, 0, 32)
+            w1_copy(k, act, 96, 128)
+            w1_copy(k, vec, 32, 64)
+            nc.vector.quantize_mx(out=w1_c[k][:].bitcast(FP8X4), scales=w1_s[k][:], in_=w1_bf[k][:])
+        for k in range(2):
+            lay(x_bf[k], x_raw[k], act, 0, 128)
+            lay(x_bf[k], x_raw[k], vec, 128, 256)
+            lay(x_bf[k], x_raw[k], vec, 256, 384)
+            lay(x_bf[k], x_raw[k], act, 384, 512)
+            quant(x_c[k], x_s[k], x_bf[k], 0, 256)
+            quant(x_c[k], x_s[k], x_bf[k], 256, 512)
+        warm_acc = [ps.tile([P, S], F32, name=f"y_acc{t}") for t in range(3)]
+        for t in range(3):
+            nc.tensor.matmul_mx(
+                out=warm_acc[t][:],
+                lhsT=w1_c[0][:, t * P : (t + 1) * P].bitcast(FP8X4),
+                lhsT_scale=w1_s[0][:, t * P : (t + 1) * P],
+                rhs=x_c[0][:].bitcast(FP8X4),
+                rhs_scale=x_s[0][:],
+                start=True,
+                stop=True,
+            )
+
+        h_acc = [ps.tile([P, 4, CH], F32, name=f"h_acc{c}") for c in range(4)]
+        for c in range(4):
+            cols = slice(c * CH, (c + 1) * CH)
             for t in range(4):
                 for k in range(2):
                     nc.tensor.matmul_mx(
-                        out=acc[:, t, :],
+                        out=h_acc[c][:, t, :],
                         lhsT=w1_c[k][:, t * P : (t + 1) * P].bitcast(FP8X4),
                         lhsT_scale=w1_s[k][:, t * P : (t + 1) * P],
-                        rhs=x_c[c][k][:].bitcast(FP8X4),
-                        rhs_scale=x_s[c][k][:],
+                        rhs=x_c[k][:, cols].bitcast(FP8X4),
+                        rhs_scale=x_s[k][:, cols],
                         start=(k == 0),
                         stop=(k == 1),
                     )
-            nc.scalar.activation(h_bf[c][:], acc[:].rearrange("p t n -> p n t"), SILU)
-
-        def h_quant(c):
-            a = (c % 2) * CH
+            nc.scalar.activation(h_bf[c][:], h_acc[c][:].rearrange("p t n -> p n t"), SILU)
             nc.vector.quantize_mx(
-                out=h_c[c // 2][:, a : a + CH].bitcast(FP8X4),
-                scales=h_s[c // 2][:, a : a + CH],
+                out=h_c[:, cols].bitcast(FP8X4),
+                scales=h_s[:, cols],
                 in_=h_bf[c][:].rearrange("p n t -> p (n t)"),
             )
+        for a in (0, 256):
+            lay(w2_bf, w2_raw, vec, a, a + 128)
+            lay(w2_bf, w2_raw, vec, a + 128, a + 256)
+            quant(w2_c, w2_s, w2_bf, a, a + 256)
 
-        def y_mm(acc, ms, t, a, n):
-            for u, m in enumerate(ms):
-                nc.tensor.matmul_mx(
-                    out=acc[:, u, :],
-                    lhsT=w2_c[m // 2][:, (m % 2) * P : (m % 2 + 1) * P].bitcast(FP8X4),
-                    lhsT_scale=w2_s[m // 2][:, (m % 2) * P : (m % 2 + 1) * P],
-                    rhs=h_c[t][:, a : a + n].bitcast(FP8X4),
-                    rhs_scale=h_s[t][:, a : a + n],
-                    start=True,
-                    stop=True,
-                )
-
-        def stage2(name, ms, t, a, n):
-            acc = ps.tile([P, len(ms), n], F32, name=f"y_acc{name}")
-            y_sb = sb.tile([P, len(ms), n], F32, name=f"y_sb{name}", align_bytes=64)
-            y_mm(acc, ms, t, a, n)
-            nc.scalar.copy(y_sb[:], acc[:])
-            j0 = t * HALF + a
-            for u, m in enumerate(ms):
-                nc.vector.tensor_tensor(
-                    win[m][:].indirect(offsets[:, j0 // 16 : (j0 + n) // 16]),
-                    y_sb[:, u, :],
-                    gate_sb[:, j0 : j0 + n],
-                    MULT,
-                )
-
-        x_prep(0, 0)
-        x_prep(0, 1)
-        stage1(0)
-        stage1(1)
-        w2_prep(0)
-        h_quant(0)
-        h_quant(1)
-        stage2("a", (0, 1), 0, 0, HALF)
-        x_prep(1, 0)
-        x_prep(1, 1)
-        stage1(2)
-        stage1(3)
-        w2_prep(1)
-        stage2("b", (2, 3), 0, 0, HALF)
-        h_quant(2)
-        stage2("c", (0, 1, 2, 3), 1, 0, CH)
-        h_quant(3)
-        stage2("d", (0, 1, 2, 3), 1, CH, CH)
-        for m in range(4):
-            nc.sync.dma_start(out=out[m * P : (m + 1) * P, :], in_=win[m][:])
+        for i, (m, j0, j1) in enumerate([(0, 0, 256), (0, 256, 512), (1, 0, 512), (2, 0, 512), (3, 0, 512)]):
+            acc = ps.tile([P, j1 - j0], F32, name=f"y_acc{i % 4}")
+            nc.tensor.matmul_mx(
+                out=acc[:],
+                lhsT=w2_c[:, m * P : (m + 1) * P].bitcast(FP8X4),
+                lhsT_scale=w2_s[:, m * P : (m + 1) * P],
+                rhs=h_c[:, j0:j1].bitcast(FP8X4),
+                rhs_scale=h_s[:, j0:j1],
+                start=True,
+                stop=True,
+            )
+            nc.scalar.copy(y_sb[m][:, j0:j1], acc[:])
+            nc.vector.tensor_tensor(
+                win[m][:].indirect(offsets[:, j0 // 16 : j1 // 16]),
+                y_sb[m][:, j0:j1],
+                gate_sb[:, j0:j1],
+                MULT,
+            )
+            if j1 == S:
+                nc.sync.dma_start(out=out[m * P : (m + 1) * P, :], in_=win[m][:])

@@ -72,12 +72,15 @@ def tile_picked_place_mlp_silu_srt_l_kernel(tc, xT, w1, w2, gate, offs, out):
 
         def w1_copy(k, copy, a, b):
             copy(
-                w1_bf[k][:].rearrange("p (t m j) -> p m t j", t=4, j=4)[:, a:b],
-                w1_raw[k][:].rearrange("p j (m t) -> p m t j", t=4)[:, a:b],
+                w1_bf[k][:].rearrange("p (t m j) -> p m j t", t=4, j=4)[:, a:b],
+                w1_raw[k][:].rearrange("p j (m t) -> p m j t", t=4)[:, a:b],
             )
 
         def lay(dst, raw, copy, a, b):
-            copy(dst[:, a:b], raw[:].rearrange("p j n -> p n j")[:, a:b])
+            copy(
+                dst[:, a:b].rearrange("p (c i) j -> p c j i", i=4),
+                raw[:, :, a:b].rearrange("p j (c i) -> p c j i", i=4),
+            )
 
         def quant(codes, scales, src, a, b):
             nc.vector.quantize_mx(
@@ -97,8 +100,8 @@ def tile_picked_place_mlp_silu_srt_l_kernel(tc, xT, w1, w2, gate, offs, out):
             lay(x_bf[k], x_raw[k], vec, 128, 256)
             lay(x_bf[k], x_raw[k], vec, 256, 384)
             lay(x_bf[k], x_raw[k], act, 384, 512)
-            quant(x_c[k], x_s[k], x_bf[k], 0, 256)
-            quant(x_c[k], x_s[k], x_bf[k], 256, 512)
+            for a in range(0, S, CH):
+                quant(x_c[k], x_s[k], x_bf[k], a, a + CH)
         warm_acc = [ps.tile([P, S], F32, name=f"y_acc{t}") for t in range(3)]
         for t in range(3):
             nc.tensor.matmul_mx(

@@ -96,23 +96,22 @@ def tile_picked_place_mlp_silu_srt_l_kernel(tc, xT, w1, w2, gate, offs, out):
             w1_copy(k, vec, 32, 64)
             nc.vector.quantize_mx(out=w1_c[k][:].bitcast(FP8X4), scales=w1_s[k][:], in_=w1_bf[k][:])
         for k in range(2):
-            lay(x_bf[k], x_raw[k], act, 0, 128)
-            lay(x_bf[k], x_raw[k], vec, 128, 256)
-            lay(x_bf[k], x_raw[k], vec, 256, 384)
-            lay(x_bf[k], x_raw[k], act, 384, 512)
+            for c, copy in enumerate((vec, act, vec, act)):
+                lay(x_bf[k], x_raw[k], copy, c * CH, (c + 1) * CH)
             for a in range(0, S, CH):
                 quant(x_c[k], x_s[k], x_bf[k], a, a + CH)
-        warm_acc = [ps.tile([P, S], F32, name=f"y_acc{t}") for t in range(3)]
-        for t in range(3):
-            nc.tensor.matmul_mx(
-                out=warm_acc[t][:],
-                lhsT=w1_c[0][:, t * P : (t + 1) * P].bitcast(FP8X4),
-                lhsT_scale=w1_s[0][:, t * P : (t + 1) * P],
-                rhs=x_c[0][:].bitcast(FP8X4),
-                rhs_scale=x_s[0][:],
-                start=True,
-                stop=True,
-            )
+        for u in range(3):
+            warm_acc = ps.tile([P, 4, CH], F32, name=f"y_acc{u}")
+            for t in range(4):
+                nc.tensor.matmul_mx(
+                    out=warm_acc[:, t, :],
+                    lhsT=w1_c[0][:, t * P : (t + 1) * P].bitcast(FP8X4),
+                    lhsT_scale=w1_s[0][:, t * P : (t + 1) * P],
+                    rhs=x_c[0][:, 0:CH].bitcast(FP8X4),
+                    rhs_scale=x_s[0][:, 0:CH],
+                    start=True,
+                    stop=True,
+                )
 
         h_acc = [ps.tile([P, 4, CH], F32, name=f"h_acc{c}") for c in range(4)]
         for c in range(4):

from contextlib import ExitStack

import concourse.mybir as mybir

K, T, S, H, N = 1024, 1024, 512, 512, 512
FLOPS = 2 * S * (K * H + H * N)
BYTES = 4 * (K * S + K * H + H * N + S + N * T) + 2 * 128 * (S // 16)

F32 = mybir.dt.float32
BF16 = mybir.dt.bfloat16
U32 = mybir.dt.uint32
U16 = mybir.dt.uint16
U8 = mybir.dt.uint8
I32 = mybir.dt.int32
FP8X4 = mybir.dt.float8_e4m3fn_x4
SILU = mybir.ActivationFunctionType.Silu
MULT = mybir.AluOpType.mult

P = 128
CH = 128
HALF = 256


def tile_picked_place_mlp_silu_srt_l_kernel(tc, xT, w1, w2, gate, offs, out):
    nc = tc.nc
    with ExitStack() as ctx:
        sb = ctx.enter_context(tc.tile_pool(name="sb", bufs=1))
        ps = ctx.enter_context(tc.psum_pool(name="ps", bufs=1))

        def tile(shape, dt, name):
            return sb.tile(shape, dt, name=name, align_bytes=64)

        offsets = sb.tile([128, S // 16], U16, name="offsets")
        gate_sb = tile([P, S], F32, "gate_sb")
        w1_raw = [tile([P, 4, H], F32, f"w1_raw{k}") for k in range(2)]
        w1_bf = [tile([P, 4 * H], BF16, f"w1_bf{k}") for k in range(2)]
        w1_c = [tile([P, H], U32, f"w1_c{k}") for k in range(2)]
        w1_s = [tile([P, H], U8, f"w1_s{k}") for k in range(2)]
        x_raw = [tile([P, 4, S], F32, f"x_raw{k}") for k in range(2)]
        x_bf = [tile([P, S, 4], BF16, f"x_bf{k}") for k in range(2)]
        x_c = [tile([P, S], U32, f"x_c{k}") for k in range(2)]
        x_s = [tile([P, S], U8, f"x_s{k}") for k in range(2)]
        w2_raw = tile([P, 4, N], F32, "w2_raw")
        w2_bf = tile([P, N, 4], BF16, "w2_bf")
        w2_c = tile([P, N], U32, "w2_c")
        w2_s = tile([P, N], U8, "w2_s")
        h_bf = [tile([P, CH, 4], BF16, f"h_bf{c}") for c in range(4)]
        h_c = tile([P, S], U32, "h_c")
        h_s = tile([P, S], U8, "h_s")
        y_sb = [tile([P, S], F32, f"y_sb{m}") for m in range(4)]
        win = [tile([P, T], F32, f"win{m}") for m in range(4)]
        warm = tile([P, 1], F32, "warm")
        warm_out = tile([P, 1], F32, "warm_out")

        def load(dst, rows):
            nc.sync.dma_start(out=dst[:], in_=rows.rearrange("(p j) n -> p j n", j=4))

        for k in range(2):
            load(w1_raw[k], w1[k * 512 : (k + 1) * 512, :])
        for k in range(2):
            load(x_raw[k], xT[k * 512 : (k + 1) * 512, :])
        load(w2_raw, w2)
        nc.sync.dma_start(offsets[:], offs)
        nc.sync.dma_start(out=gate_sb[:], in_=gate[0:P, :])

        nc.gpsimd.memset(warm[:], 0.0)
        nc.scalar.activation(warm_out[:], warm[:], SILU)
        for m in range(4):
            nc.vector.memset(win[m][:].bitcast(I32), 0)

        act, vec = nc.scalar.copy, nc.vector.tensor_copy

        def w1_copy(k, copy, a, b):
            copy(
                w1_bf[k][:].rearrange("p (t m j) -> p m j t", t=4, j=4)[:, a:b],
                w1_raw[k][:].rearrange("p j (m t) -> p m j t", t=4)[:, a:b],
            )

        def lay(dst, raw, copy, a, b):
            copy(
                dst[:, a:b].rearrange("p (c i) j -> p c j i", i=4),
                raw[:, :, a:b].rearrange("p j (c i) -> p c j i", i=4),
            )

        def quant(codes, scales, src, a, b):
            nc.vector.quantize_mx(
                out=codes[:, a:b].bitcast(FP8X4),
                scales=scales[:, a:b],
                in_=src[:, a:b].rearrange("p n j -> p (n j)"),
            )

        for k in range(2):
            w1_copy(k, act, 64, 96)
            w1_copy(k, vec, 0, 32)
            w1_copy(k, act, 96, 128)
            w1_copy(k, vec, 32, 64)
            nc.vector.quantize_mx(out=w1_c[k][:].bitcast(FP8X4), scales=w1_s[k][:], in_=w1_bf[k][:])
        for k in range(2):
            for c, copy in enumerate((vec, act, vec, act)):
                lay(x_bf[k], x_raw[k], copy, c * CH, (c + 1) * CH)
            for a in range(0, S, CH):
                quant(x_c[k], x_s[k], x_bf[k], a, a + CH)
        for u in range(3):
            warm_acc = ps.tile([P, 4, CH], F32, name=f"y_acc{u}")
            for t in range(4):
                nc.tensor.matmul_mx(
                    out=warm_acc[:, t, :],
                    lhsT=w1_c[0][:, t * P : (t + 1) * P].bitcast(FP8X4),
                    lhsT_scale=w1_s[0][:, t * P : (t + 1) * P],
                    rhs=x_c[0][:, 0:CH].bitcast(FP8X4),
                    rhs_scale=x_s[0][:, 0:CH],
                    start=True,
                    stop=True,
                )

        h_acc = [ps.tile([P, 4, CH], F32, name=f"h_acc{c}") for c in range(4)]
        for c in range(4):
            cols = slice(c * CH, (c + 1) * CH)
            for t in range(4):
                for k in range(2):
                    nc.tensor.matmul_mx(
                        out=h_acc[c][:, t, :],
                        lhsT=w1_c[k][:, t * P : (t + 1) * P].bitcast(FP8X4),
                        lhsT_scale=w1_s[k][:, t * P : (t + 1) * P],
                        rhs=x_c[k][:, cols].bitcast(FP8X4),
                        rhs_scale=x_s[k][:, cols],
                        start=(k == 0),
                        stop=(k == 1),
                    )
            nc.scalar.activation(h_bf[c][:], h_acc[c][:].rearrange("p t n -> p n t"), SILU)
            nc.vector.quantize_mx(
                out=h_c[:, cols].bitcast(FP8X4),
                scales=h_s[:, cols],
                in_=h_bf[c][:].rearrange("p n t -> p (n t)"),
            )
        for a in (0, 256):
            lay(w2_bf, w2_raw, vec, a, a + 128)
            lay(w2_bf, w2_raw, vec, a + 128, a + 256)
            quant(w2_c, w2_s, w2_bf, a, a + 256)

        for i, (m, j0, j1) in enumerate([(0, 0, 256), (0, 256, 512), (1, 0, 512), (2, 0, 512), (3, 0, 512)]):
            acc = ps.tile([P, j1 - j0], F32, name=f"y_acc{i % 4}")
            nc.tensor.matmul_mx(
                out=acc[:],
                lhsT=w2_c[:, m * P : (m + 1) * P].bitcast(FP8X4),
                lhsT_scale=w2_s[:, m * P : (m + 1) * P],
                rhs=h_c[:, j0:j1].bitcast(FP8X4),
                rhs_scale=h_s[:, j0:j1],
                start=True,
                stop=True,
            )
            nc.scalar.copy(y_sb[m][:, j0:j1], acc[:])
            nc.vector.tensor_tensor(
                win[m][:].indirect(offsets[:, j0 // 16 : j1 // 16]),
                y_sb[m][:, j0:j1],
                gate_sb[:, j0:j1],
                MULT,
            )
            if j1 == S:
                nc.sync.dma_start(out=out[m * P : (m + 1) * P, :], in_=win[m][:])
